import numpy as np
import ml_dtypes

BF16 = ml_dtypes.bfloat16


def bf(x):
    return np.asarray(x, np.float32).astype(BF16)


def f32(x):
    return np.asarray(x, np.float32)


def f64(x):
    return np.asarray(x).astype(np.float64)


def striped(idx):
    return np.concatenate([l.reshape(-1, 16).T for l in idx])


def rows(idx, k):
    return np.tile(np.repeat(idx, 16, axis=0), (k // (16 * 8), 1))


def look(tab, idx):
    return np.take_along_axis(f64(tab), rows(idx, len(tab)), axis=1)


K, S, H, V, N, M = 128, 2048, 256, 512, 512, 512


def setup_inputs():
    return {"z": bf(np.random.standard_normal((H, S))), "wt": bf(np.random.standard_normal((H, K)) / np.sqrt(H)), "y": f32(1.0 * np.random.standard_normal((K, V))), "w": bf(np.random.standard_normal((K, M)) / np.sqrt(K)), "b": f32(0.5 * np.random.standard_normal((M, 1))), "offs": striped(np.stack([np.random.permutation(S)[:N] for _ in range(8)]))}


def reference(z, wt, y, w, b, offs):
    idx = np.stack([g.T.reshape(-1) for g in np.split(offs, 8)])
    tab = f64(wt).T @ f64(z)
    x = f64(y) / (1.0 + np.exp(-look(tab, idx)))
    return np.maximum(f64(w).T @ x + f64(b), 0.0)

@@ -1,0 +1,81 @@
+import concourse.mybir as mybir
+
+BF16, F32, U16 = mybir.dt.bfloat16, mybir.dt.float32, mybir.dt.uint16
+ACT = mybir.ActivationFunctionType
+ALU = mybir.AluOpType
+
+P = 128
+K_BLOCKS = 2
+PLACES = 2048
+N = 512
+M = 512
+M_PER_ROW = M // P
+CHUNK = 512
+PIECE = CHUNK // 2
+
+FLOPS = 2 * K_BLOCKS * P * P * PLACES + 2 * P * M * N
+
+
+def tile_lookup_pjsig_relu_kernel(tc, z, wt, y, w, b, offs, out):
+    nc = tc.nc
+    with (
+        tc.tile_pool(name="held", bufs=1) as held,
+        tc.psum_pool(name="psum", bufs=8) as psum,
+    ):
+        wt_tile = held.tile([P, K_BLOCKS, P], BF16, name="wt_tile")
+        nc.scalar.dma_start(wt_tile[:], wt.rearrange("(k p) r -> p k r", p=P))
+        z_rows = z.rearrange("(k p) s -> p k s", p=P)
+        z_tiles = []
+        for c in range(PLACES // CHUNK):
+            z_tile = held.tile([P, K_BLOCKS, CHUNK], BF16, name=f"z_tile{c}")
+            nc.sync.dma_start(z_tile[:], z_rows[:, :, c * CHUNK : (c + 1) * CHUNK])
+            z_tiles.append(z_tile)
+        offsets = held.tile([P, N // 16], U16, name="offsets")
+        nc.sync.dma_start(offsets[:], offs)
+        y_tile = held.tile([P, N], F32, name="y_tile")
+        nc.sync.dma_start(y_tile[:], y)
+        w_tile = held.tile([P, M], BF16, name="w_tile")
+        nc.scalar.dma_start(w_tile[:], w)
+        b_tile = held.tile([P, M_PER_ROW], F32, name="b_tile")
+        nc.scalar.dma_start(b_tile[:], b.rearrange("(p q) o -> p (q o)", q=M_PER_ROW))
+
+        table = held.tile([P, PLACES], F32, name="table")
+        for c in range(PLACES // CHUNK):
+            for half in range(2):
+                scores = psum.tile([P, PIECE], F32, name="scores", tag="bank")
+                for k in range(K_BLOCKS):
+                    nc.tensor.matmul(
+                        scores[:],
+                        wt_tile[:, k, :],
+                        z_tiles[c][:, k, half * PIECE : (half + 1) * PIECE],
+                        start=k == 0,
+                        stop=k == K_BLOCKS - 1,
+                    )
+                start = c * CHUNK + half * PIECE
+                if half == 0:
+                    nc.vector.tensor_copy(table[:, start : start + PIECE], scores[:])
+                else:
+                    nc.scalar.copy(table[:, start : start + PIECE], scores[:])
+
+        gates = held.tile([P, N], F32, name="gates")
+        nc.scalar.activation(gates[:], table[:].indirect(offsets[:]), ACT.Sigmoid)
+
+        x = held.tile([P, N], BF16, name="x")
+        for half in range(2):
+            columns = slice(half * PIECE, (half + 1) * PIECE)
+            nc.vector.tensor_tensor(x[:, columns], gates[:, columns], y_tile[:, columns], ALU.mult)
+
+        w_by_q = w_tile[:].rearrange("r (p q) -> r q p", q=M_PER_ROW)
+        out_rows = out.rearrange("(p q) j -> p q j", q=M_PER_ROW)
+        result = held.tile([P, M_PER_ROW, N], F32, name="result")
+        for half in range(2):
+            columns = slice(half * PIECE, (half + 1) * PIECE)
+            for q in range(M_PER_ROW):
+                layer = psum.tile([P, PIECE], F32, name="layer", tag="bank")
+                nc.tensor.matmul(layer[:], w_by_q[:, q, :], x[:, columns], start=True, stop=True)
+                bias = b_tile[:, q : q + 1]
+                if q % 2 == 0:
+                    nc.scalar.activation(result[:, q, columns], layer[:], ACT.Relu, bias=bias)
+                else:
+                    nc.vector.tensor_scalar(result[:, q, columns], layer[:], bias, 0.0, ALU.add, ALU.max)
+                    nc.sync.dma_start(out_rows[:, q - 1 : q + 1, columns], result[:, q - 1 : q + 1, columns])

@@ -11,6 +11,7 @@ N = 512
 M = 512
 M_PER_ROW = M // P
 CHUNK = 512
+WARM_UPS = 6
 PIECE = CHUNK // 2
 
 FLOPS = 2 * K_BLOCKS * P * P * PLACES + 2 * P * M * N
@@ -22,6 +23,12 @@ def tile_lookup_pjsig_relu_kernel(tc, z, wt, y, w, b, offs, out):
         tc.tile_pool(name="held", bufs=1) as held,
         tc.psum_pool(name="psum", bufs=8) as psum,
     ):
+        zeros = held.tile([P, N], BF16, name="zeros")
+        nc.vector.memset(zeros[:], 0.0)
+        for i in range(WARM_UPS):
+            warm = psum.tile([P, N], F32, name="warm", tag="bank")
+            nc.tensor.matmul(warm[:], zeros[:, :P], zeros[:], start=True, stop=True)
+
         wt_tile = held.tile([P, K_BLOCKS, P], BF16, name="wt_tile")
         nc.scalar.dma_start(wt_tile[:], wt.rearrange("(k p) r -> p k r", p=P))
         z_rows = z.rearrange("(k p) s -> p k s", p=P)
@@ -38,6 +45,11 @@ def tile_lookup_pjsig_relu_kernel(tc, z, wt, y, w, b, offs, out):
         nc.scalar.dma_start(w_tile[:], w)
         b_tile = held.tile([P, M_PER_ROW], F32, name="b_tile")
         nc.scalar.dma_start(b_tile[:], b.rearrange("(p q) o -> p (q o)", q=M_PER_ROW))
+
+        first_in = held.tile([P, 1], F32, name="first_in")
+        nc.vector.memset(first_in[:], 0.0)
+        first_out = held.tile([P, 1], F32, name="first_out")
+        nc.scalar.activation(first_out[:], first_in[:], ACT.Sigmoid)
 
         table = held.tile([P, PLACES], F32, name="table")
         for c in range(PLACES // CHUNK):

@@ -11,7 +11,8 @@ N = 512
 M = 512
 M_PER_ROW = M // P
 CHUNK = 512
-WARM_UPS = 6
+WARM_UPS = 4
+KEEP_UPS = 5
 PIECE = CHUNK // 2
 
 FLOPS = 2 * K_BLOCKS * P * P * PLACES + 2 * P * M * N
@@ -21,12 +22,13 @@ def tile_lookup_pjsig_relu_kernel(tc, z, wt, y, w, b, offs, out):
     nc = tc.nc
     with (
         tc.tile_pool(name="held", bufs=1) as held,
-        tc.psum_pool(name="psum", bufs=8) as psum,
+        tc.psum_pool(name="psum", bufs=7) as psum,
+        tc.psum_pool(name="spare", bufs=1) as spare,
     ):
         zeros = held.tile([P, N], BF16, name="zeros")
         nc.vector.memset(zeros[:], 0.0)
+        warm = spare.tile([P, N], F32, name="warm")
         for i in range(WARM_UPS):
-            warm = psum.tile([P, N], F32, name="warm", tag="bank")
             nc.tensor.matmul(warm[:], zeros[:, :P], zeros[:], start=True, stop=True)
 
         wt_tile = held.tile([P, K_BLOCKS, P], BF16, name="wt_tile")
@@ -34,17 +36,19 @@ def tile_lookup_pjsig_relu_kernel(tc, z, wt, y, w, b, offs, out):
         z_rows = z.rearrange("(k p) s -> p k s", p=P)
         z_tiles = []
         for c in range(PLACES // CHUNK):
-            z_tile = held.tile([P, K_BLOCKS, CHUNK], BF16, name=f"z_tile{c}")
-            nc.sync.dma_start(z_tile[:], z_rows[:, :, c * CHUNK : (c + 1) * CHUNK])
-            z_tiles.append(z_tile)
+            z_tiles.append([])
+            for k in range(K_BLOCKS):
+                z_tile = held.tile([P, CHUNK], BF16, name=f"z_tile{c}_{k}")
+                nc.sync.dma_start(z_tile[:], z_rows[:, k, c * CHUNK : (c + 1) * CHUNK])
+                z_tiles[c].append(z_tile)
         offsets = held.tile([P, N // 16], U16, name="offsets")
         nc.sync.dma_start(offsets[:], offs)
         y_tile = held.tile([P, N], F32, name="y_tile")
         nc.sync.dma_start(y_tile[:], y)
         w_tile = held.tile([P, M], BF16, name="w_tile")
-        nc.scalar.dma_start(w_tile[:], w)
+        nc.sync.dma_start(w_tile[:], w)
         b_tile = held.tile([P, M_PER_ROW], F32, name="b_tile")
-        nc.scalar.dma_start(b_tile[:], b.rearrange("(p q) o -> p (q o)", q=M_PER_ROW))
+        nc.sync.dma_start(b_tile[:], b.rearrange("(p q) o -> p (q o)", q=M_PER_ROW))
 
         first_in = held.tile([P, 1], F32, name="first_in")
         nc.vector.memset(first_in[:], 0.0)
@@ -53,21 +57,18 @@ def tile_lookup_pjsig_relu_kernel(tc, z, wt, y, w, b, offs, out):
 
         table = held.tile([P, PLACES], F32, name="table")
         for c in range(PLACES // CHUNK):
-            for half in range(2):
-                scores = psum.tile([P, PIECE], F32, name="scores", tag="bank")
-                for k in range(K_BLOCKS):
-                    nc.tensor.matmul(
-                        scores[:],
-                        wt_tile[:, k, :],
-                        z_tiles[c][:, k, half * PIECE : (half + 1) * PIECE],
-                        start=k == 0,
-                        stop=k == K_BLOCKS - 1,
-                    )
-                start = c * CHUNK + half * PIECE
-                if half == 0:
-                    nc.vector.tensor_copy(table[:, start : start + PIECE], scores[:])
-                else:
-                    nc.scalar.copy(table[:, start : start + PIECE], scores[:])
+            left = psum.tile([P, PIECE], F32, name="left", tag="bank")
+            right = psum.tile([P, PIECE], F32, name="right", tag="bank")
+            for k in range(K_BLOCKS):
+                first, last = k == 0, k == K_BLOCKS - 1
+                nc.tensor.matmul(left[:], wt_tile[:, k, :], z_tiles[c][k][:, :PIECE], start=first, stop=last)
+                nc.tensor.matmul(right[:], wt_tile[:, k, :], z_tiles[c][k][:, PIECE:], start=first, stop=last)
+            start = c * CHUNK
+            nc.vector.tensor_copy(table[:, start : start + PIECE], left[:])
+            nc.scalar.copy(table[:, start + PIECE : start + CHUNK], right[:])
+
+        for i in range(KEEP_UPS):
+            nc.tensor.matmul(warm[:], wt_tile[:, 0, :], z_tiles[-1][-1][:], start=True, stop=True)
 
         gates = held.tile([P, N], F32, name="gates")
         nc.scalar.activation(gates[:], table[:].indirect(offsets[:]), ACT.Sigmoid)

@@ -11,7 +11,7 @@ N = 512
 M = 512
 M_PER_ROW = M // P
 CHUNK = 512
-WARM_UPS = 4
+WARM_UPS = 14
 KEEP_UPS = 5
 PIECE = CHUNK // 2
 
@@ -25,11 +25,11 @@ def tile_lookup_pjsig_relu_kernel(tc, z, wt, y, w, b, offs, out):
         tc.psum_pool(name="psum", bufs=7) as psum,
         tc.psum_pool(name="spare", bufs=1) as spare,
     ):
-        zeros = held.tile([P, N], BF16, name="zeros")
+        zeros = held.tile([P, P], BF16, name="zeros")
         nc.vector.memset(zeros[:], 0.0)
         warm = spare.tile([P, N], F32, name="warm")
         for i in range(WARM_UPS):
-            nc.tensor.matmul(warm[:], zeros[:, :P], zeros[:], start=True, stop=True)
+            nc.tensor.matmul(warm[:, :P], zeros[:], zeros[:], start=True, stop=True)
 
         wt_tile = held.tile([P, K_BLOCKS, P], BF16, name="wt_tile")
         nc.scalar.dma_start(wt_tile[:], wt.rearrange("(k p) r -> p k r", p=P))
@@ -91,4 +91,4 @@ def tile_lookup_pjsig_relu_kernel(tc, z, wt, y, w, b, offs, out):
                     nc.scalar.activation(result[:, q, columns], layer[:], ACT.Relu, bias=bias)
                 else:
                     nc.vector.tensor_scalar(result[:, q, columns], layer[:], bias, 0.0, ALU.add, ALU.max)
-                    nc.sync.dma_start(out_rows[:, q - 1 : q + 1, columns], result[:, q - 1 : q + 1, columns])
+                nc.sync.dma_start(out_rows[:, q, columns], result[:, q, columns])

@@ -43,10 +43,10 @@ def tile_lookup_pjsig_relu_kernel(tc, z, wt, y, w, b, offs, out):
                 z_tiles[c].append(z_tile)
         offsets = held.tile([P, N // 16], U16, name="offsets")
         nc.sync.dma_start(offsets[:], offs)
-        y_tile = held.tile([P, N], F32, name="y_tile")
-        nc.sync.dma_start(y_tile[:], y)
         w_tile = held.tile([P, M], BF16, name="w_tile")
         nc.sync.dma_start(w_tile[:], w)
+        y_tile = held.tile([P, N], F32, name="y_tile")
+        nc.sync.dma_start(y_tile[:], y)
         b_tile = held.tile([P, M_PER_ROW], F32, name="b_tile")
         nc.sync.dma_start(b_tile[:], b.rearrange("(p q) o -> p (q o)", q=M_PER_ROW))
 
@@ -73,12 +73,13 @@ def tile_lookup_pjsig_relu_kernel(tc, z, wt, y, w, b, offs, out):
         gates = held.tile([P, N], F32, name="gates")
         nc.scalar.activation(gates[:], table[:].indirect(offsets[:]), ACT.Sigmoid)
 
+        w_by_q = held.tile([P, M_PER_ROW, P], BF16, name="w_by_q")
+        nc.vector.tensor_copy(w_by_q[:], w_tile[:].rearrange("r (p q) -> r q p", q=M_PER_ROW))
         x = held.tile([P, N], BF16, name="x")
         for half in range(2):
             columns = slice(half * PIECE, (half + 1) * PIECE)
             nc.vector.tensor_tensor(x[:, columns], gates[:, columns], y_tile[:, columns], ALU.mult)
 
-        w_by_q = w_tile[:].rearrange("r (p q) -> r q p", q=M_PER_ROW)
         out_rows = out.rearrange("(p q) j -> p q j", q=M_PER_ROW)
         result = held.tile([P, M_PER_ROW, N], F32, name="result")
         for half in range(2):

import concourse.mybir as mybir

BF16, F32, U16 = mybir.dt.bfloat16, mybir.dt.float32, mybir.dt.uint16
ACT = mybir.ActivationFunctionType
ALU = mybir.AluOpType

P = 128
K_BLOCKS = 2
PLACES = 2048
N = 512
M = 512
M_PER_ROW = M // P
CHUNK = 512
WARM_UPS = 14
KEEP_UPS = 5
PIECE = CHUNK // 2

FLOPS = 2 * K_BLOCKS * P * P * PLACES + 2 * P * M * N


def tile_lookup_pjsig_relu_kernel(tc, z, wt, y, w, b, offs, out):
    nc = tc.nc
    with (
        tc.tile_pool(name="held", bufs=1) as held,
        tc.psum_pool(name="psum", bufs=7) as psum,
        tc.psum_pool(name="spare", bufs=1) as spare,
    ):
        zeros = held.tile([P, P], BF16, name="zeros")
        nc.vector.memset(zeros[:], 0.0)
        warm = spare.tile([P, N], F32, name="warm")
        for i in range(WARM_UPS):
            nc.tensor.matmul(warm[:, :P], zeros[:], zeros[:], start=True, stop=True)

        wt_tile = held.tile([P, K_BLOCKS, P], BF16, name="wt_tile")
        nc.scalar.dma_start(wt_tile[:], wt.rearrange("(k p) r -> p k r", p=P))
        z_rows = z.rearrange("(k p) s -> p k s", p=P)
        z_tiles = []
        for c in range(PLACES // CHUNK):
            z_tiles.append([])
            for k in range(K_BLOCKS):
                z_tile = held.tile([P, CHUNK], BF16, name=f"z_tile{c}_{k}")
                nc.sync.dma_start(z_tile[:], z_rows[:, k, c * CHUNK : (c + 1) * CHUNK])
                z_tiles[c].append(z_tile)
        offsets = held.tile([P, N // 16], U16, name="offsets")
        nc.sync.dma_start(offsets[:], offs)
        w_tile = held.tile([P, M], BF16, name="w_tile")
        nc.sync.dma_start(w_tile[:], w)
        y_tile = held.tile([P, N], F32, name="y_tile")
        nc.sync.dma_start(y_tile[:], y)
        b_tile = held.tile([P, M_PER_ROW], F32, name="b_tile")
        nc.sync.dma_start(b_tile[:], b.rearrange("(p q) o -> p (q o)", q=M_PER_ROW))

        first_in = held.tile([P, 1], F32, name="first_in")
        nc.vector.memset(first_in[:], 0.0)
        first_out = held.tile([P, 1], F32, name="first_out")
        nc.scalar.activation(first_out[:], first_in[:], ACT.Sigmoid)

        table = held.tile([P, PLACES], F32, name="table")
        for c in range(PLACES // CHUNK):
            left = psum.tile([P, PIECE], F32, name="left", tag="bank")
            right = psum.tile([P, PIECE], F32, name="right", tag="bank")
            for k in range(K_BLOCKS):
                first, last = k == 0, k == K_BLOCKS - 1
                nc.tensor.matmul(left[:], wt_tile[:, k, :], z_tiles[c][k][:, :PIECE], start=first, stop=last)
                nc.tensor.matmul(right[:], wt_tile[:, k, :], z_tiles[c][k][:, PIECE:], start=first, stop=last)
            start = c * CHUNK
            nc.vector.tensor_copy(table[:, start : start + PIECE], left[:])
            nc.scalar.copy(table[:, start + PIECE : start + CHUNK], right[:])

        for i in range(KEEP_UPS):
            nc.tensor.matmul(warm[:], wt_tile[:, 0, :], z_tiles[-1][-1][:], start=True, stop=True)

        gates = held.tile([P, N], F32, name="gates")
        nc.scalar.activation(gates[:], table[:].indirect(offsets[:]), ACT.Sigmoid)

        w_by_q = held.tile([P, M_PER_ROW, P], BF16, name="w_by_q")
        nc.vector.tensor_copy(w_by_q[:], w_tile[:].rearrange("r (p q) -> r q p", q=M_PER_ROW))
        x = held.tile([P, N], BF16, name="x")
        for half in range(2):
            columns = slice(half * PIECE, (half + 1) * PIECE)
            nc.vector.tensor_tensor(x[:, columns], gates[:, columns], y_tile[:, columns], ALU.mult)

        out_rows = out.rearrange("(p q) j -> p q j", q=M_PER_ROW)
        result = held.tile([P, M_PER_ROW, N], F32, name="result")
        for half in range(2):
            columns = slice(half * PIECE, (half + 1) * PIECE)
            for q in range(M_PER_ROW):
                layer = psum.tile([P, PIECE], F32, name="layer", tag="bank")
                nc.tensor.matmul(layer[:], w_by_q[:, q, :], x[:, columns], start=True, stop=True)
                bias = b_tile[:, q : q + 1]
                if q % 2 == 0:
                    nc.scalar.activation(result[:, q, columns], layer[:], ACT.Relu, bias=bias)
                else:
                    nc.vector.tensor_scalar(result[:, q, columns], layer[:], bias, 0.0, ALU.add, ALU.max)
                nc.sync.dma_start(out_rows[:, q, columns], result[:, q, columns])
